import numpy as np
import ml_dtypes


def mxq(x, axis, fmt="e4m3"):
    dtype, down = {"e4m3": (ml_dtypes.float8_e4m3fn, 7), "e5m2": (ml_dtypes.float8_e5m2, 14)}[fmt]
    v = np.moveaxis(np.asarray(x, np.float32).astype(ml_dtypes.bfloat16).astype(np.float64), axis, -1)
    blocks = v.reshape(v.shape[:-1] + (-1, 32))
    amax = np.abs(blocks).max(-1, keepdims=True)
    byte = np.maximum(np.where(amax > 0, np.frexp(amax)[1] - 1 + 127, 0) - down, 1)
    scale = np.exp2(byte - 127.0)
    codes = (blocks / scale).astype(np.float32).astype(dtype).astype(np.float64)
    return np.moveaxis((codes * scale).reshape(v.shape), -1, axis)


WIDE = False


def mx_kscale(k):
    if not WIDE:
        return np.ones(k)
    levels = np.array([24, -24, 12, -12, 0])
    if k % 512:
        return np.exp2(np.random.permutation(np.resize(levels, k // 32))).repeat(32)
    a = np.empty((k // 512, 16))
    for p in range(k // 512):
        a[p, :8] = np.random.permutation(np.resize(levels, 8))
        for g in range(8):
            far = levels[np.abs(levels - a[p, g]) >= 10]
            a[p, g + 8] = far[np.random.randint(len(far))]
    return np.exp2(a.ravel()).repeat(32)


def f64(x):
    return np.asarray(x).astype(np.float64)


def striped(idx):
    return np.tile(idx.reshape(-1, 16).T, (8, 1)).astype(np.uint16)


def unstriped(offs):
    return offs[:16].T.reshape(-1).astype(np.int64)


E2M1 = np.array([0.0, 0.5, 1.0, 1.5, 2.0, 3.0, 4.0, 6.0, -0.0, -0.5, -1.0, -1.5, -2.0, -3.0, -4.0, -6.0])


def pack_weight(w, fmt):
    k, n = w.shape
    w = f64(np.asarray(w, np.float32).astype(ml_dtypes.bfloat16)).reshape(k // 32, 32, n)
    amax = np.abs(w).max(1)
    if fmt == "e4m3":
        byte = np.frexp(amax)[1] - 1 + 127 - 7
    else:
        mant, ex = np.frexp(amax / 6.0)
        byte = np.where(mant > 0.5, ex, ex - 1) + 127
    byte = np.clip(np.where(amax > 0, byte, 1), 1, 254)
    scaled = (w * np.exp2(127.0 - byte)[:, None, :]).reshape(k, n).astype(np.float32)
    by_word = np.ascontiguousarray(scaled.reshape(k // 512, 128, 4, n).transpose(0, 1, 3, 2))
    if fmt == "e4m3":
        words = by_word.astype(ml_dtypes.float8_e4m3fn).view(np.uint8)
    else:
        c = by_word.astype(ml_dtypes.float4_e2m1fn).view(np.uint8) & 0xF
        words = (c[..., 0::2] | (c[..., 1::2] << 4)).reshape(k // 512, 128, 2 * n)
    return np.ascontiguousarray(words), np.ascontiguousarray(byte.astype(np.uint8).reshape(k // 512, 16, n))


def unpack_weight(words, scales, fmt):
    g, _, n = scales.shape
    words = np.ascontiguousarray(words).reshape(g, 128, n, -1)
    if fmt == "e4m3":
        vals = words.view(ml_dtypes.float8_e4m3fn).astype(np.float64)
    else:
        nib = np.empty((g, 128, n, 4), np.uint8)
        nib[..., 0::2] = words & 0xF
        nib[..., 1::2] = words >> 4
        vals = E2M1[nib]
    vals = vals * np.repeat(np.exp2(scales.astype(np.float64) - 127.0), 8, axis=1)[..., None]
    return vals.transpose(0, 1, 3, 2).reshape(g * 512, n)


def gelu(f):
    return 0.5 * f * (1.0 + np.tanh(np.sqrt(2.0 / np.pi) * (f + 0.044715 * f**3)))


K, M, N, J, T = 512, 1024, 256, 2048, 4096


def setup_inputs():
    n = np.random.standard_normal
    s = mx_kscale(K)[:, None]
    u = mx_kscale(J)[:, None]
    al = n((J, N)) / np.sqrt(J) / u
    al4 = pack_weight(al, "e2m1")
    alrest = al - unpack_weight(*al4, "e2m1")
    p_tab = pack_weight(0.5 * n((K, T)) / np.sqrt(K) / s, "e4m3")
    p_al8 = pack_weight(alrest, "e4m3")
    return {
        "x": (n((K, M)) * s).astype(np.float32),
        "tab_words": p_tab[0],
        "tab_scales": p_tab[1],
        "cw": (np.random.uniform(0.5, 2.0, J) * u[:, 0]).astype(np.float32),
        "cb": (0.3 * n(J)).astype(np.float32),
        "al4_words": al4[0],
        "al4_scales": al4[1],
        "al8_words": p_al8[0],
        "al8_scales": p_al8[1],
        "b": (0.3 * n(N)).astype(np.float32),
        "offs": striped(np.random.permutation(T)[:J]),
    }


def reference(x, tab_words, tab_scales, cw, cb, al4_words, al4_scales, al8_words, al8_scales, b, offs):
    idx = unstriped(offs)
    x_ = mxq(f64(x), 0, "e4m3")
    tab_ = unpack_weight(tab_words, tab_scales, "e4m3")[:, idx]
    d = tab_.T @ x_
    h = f64(cw)[:, None] * np.exp(d - f64(cb)[:, None])
    h_ = mxq(h, 0, "e4m3")
    al4_ = unpack_weight(al4_words, al4_scales, "e2m1")
    al8_ = unpack_weight(al8_words, al8_scales, "e4m3")
    y = al4_.T @ h_ + al8_.T @ h_
    return gelu(y + f64(b)[:, None])

@@ -1,0 +1,211 @@
+from contextlib import ExitStack
+
+import concourse.mybir as mybir
+
+K, M, N, J, T = 512, 1024, 256, 2048, 4096
+FLOPS = 2 * K * J * M + 2 * 2 * J * N * M
+
+F32 = mybir.dt.float32
+BF16 = mybir.dt.bfloat16
+I32 = mybir.dt.int32
+U32 = mybir.dt.uint32
+U16 = mybir.dt.uint16
+U8 = mybir.dt.uint8
+FP8X4 = mybir.dt.float8_e4m3fn_x4
+FP4X4 = mybir.dt.float4_e2m1fn_x4
+ACT = mybir.ActivationFunctionType
+ALU = mybir.AluOpType
+
+P = 128
+PACK = 4
+PASS = P * PACK
+J_PASSES = J // PASS
+M_TILE = 512
+M_TILES = M // M_TILE
+N_TILES = N // P
+LIST_COLS = PASS // 16
+
+SIGN_AND_EXPONENT = -(1 << 23)
+MANTISSA = (1 << 23) - 1
+ONE_BITS = 127 << 23
+
+
+def tile_list_kernl_exp_res_gelu_kernel(
+    tc, x, tab_words, tab_scales, cw, cb, al4_words, al4_scales, al8_words, al8_scales, b, offs, out
+):
+    nc = tc.nc
+    with ExitStack() as ctx:
+        keep = ctx.enter_context(tc.tile_pool(name="keep", bufs=1))
+        ring = ctx.enter_context(tc.tile_pool(name="ring", bufs=1))
+        psum = ctx.enter_context(tc.psum_pool(name="psum", bufs=1))
+
+        offsets = keep.tile([P, J // 16], U16, name="offsets")
+        nc.sync.dma_start(offsets[:], offs)
+
+        tab_s = keep.tile([P, T], U8, name="tab_s", align_bytes=64)
+        nc.vector.memset(tab_s[:].bitcast(I32), 0)
+        for q in range(4):
+            nc.sync.dma_start(
+                tab_s[32 * q : 32 * q + 4, :].bitcast(I32), tab_scales[0, 4 * q : 4 * q + 4, :].bitcast(I32)
+            )
+
+        cw_t = keep.tile([P, J_PASSES, PACK], F32, name="cw_t")
+        cb_t = keep.tile([P, J_PASSES, PACK], F32, name="cb_t")
+        nc.sync.dma_start(cw_t[:], cw.rearrange("(a p t) -> p a t", p=P, t=PACK))
+        nc.sync.dma_start(cb_t[:], cb.rearrange("(a p t) -> p a t", p=P, t=PACK))
+
+        x_view = x.rearrange("(p t) m -> p t m", t=PACK)
+        x_raw = [keep.tile([P, PACK, M_TILE], F32, name=f"x_raw{mt}", align_bytes=64) for mt in range(M_TILES)]
+        tab_w = keep.tile([P, T], I32, name="tab_w", align_bytes=64)
+        nc.sync.dma_start(x_raw[0][:], x_view[:, :, 0:M_TILE])
+        nc.sync.dma_start(tab_w[:], tab_words[0].rearrange("p t i -> p (t i)").bitcast(I32))
+
+        al4_s = keep.tile([P, J_PASSES, N], U8, name="al4_s", align_bytes=64)
+        al8_s = keep.tile([P, J_PASSES, N], U8, name="al8_s", align_bytes=64)
+        nc.gpsimd.memset(al4_s[:].bitcast(I32), 0)
+        nc.gpsimd.memset(al8_s[:].bitcast(I32), 0)
+        al8_w = keep.tile([P, J_PASSES, N], I32, name="al8_w", align_bytes=64)
+        al4_w = keep.tile([P, J_PASSES, N // 2], I32, name="al4_w", align_bytes=64)
+        nc.sync.dma_start(al8_w[:], al8_words.rearrange("a p n i -> p a (n i)").bitcast(I32))
+        nc.sync.dma_start(al4_w[:], al4_words.rearrange("a p c -> p a c").bitcast(I32))
+        for plane, rows in ((al4_s, al4_scales), (al8_s, al8_scales)):
+            for q in range(4):
+                nc.sync.dma_start(
+                    plane[32 * q : 32 * q + 4, :, :].bitcast(I32),
+                    rows[:, 4 * q : 4 * q + 4, :].rearrange("a r n -> r a n").bitcast(I32),
+                )
+        nc.sync.dma_start(x_raw[1][:], x_view[:, :, M_TILE:M])
+        b_t = keep.tile([P, N_TILES], F32, name="b_t")
+        with nc.allow_non_contiguous_dma(reason="one bias value a partition"):
+            nc.sync.dma_start(b_t[:], b.rearrange("(u p) -> p u", p=P))
+
+        cw_bits = cw_t[:].rearrange("p a t -> p (a t)").bitcast(I32)
+        power = keep.tile([P, J_PASSES * PACK], F32, name="power")
+        mant = keep.tile([P, J_PASSES * PACK], F32, name="mant")
+        nc.vector.tensor_scalar(mant[:].bitcast(I32), cw_bits, MANTISSA, ONE_BITS, ALU.bitwise_and, ALU.bitwise_or)
+        nc.vector.tensor_scalar(power[:].bitcast(I32), cw_bits, SIGN_AND_EXPONENT, None, ALU.bitwise_and)
+        log_mant = keep.tile([P, J_PASSES * PACK], F32, name="log_mant")
+        nc.scalar.activation(log_mant[:], mant[:], ACT.Ln)
+        results = [keep.tile([P, N_TILES, M_TILE], F32, name=f"result{mt}") for mt in range(M_TILES)]
+        shift = results[0][:, :, 0 : J_PASSES * PACK // N_TILES].rearrange("p u c -> p c u")
+        nc.vector.tensor_tensor(
+            shift,
+            log_mant[:].rearrange("p (c u) -> p c u", u=N_TILES),
+            cb_t[:].rearrange("p a (c u) -> p (a c) u", u=N_TILES),
+            ALU.subtract,
+        )
+
+        def gather_scales(a):
+            picked = ring.tile([P, PASS], U8, name="picked_s", bufs=2, align_bytes=64)
+            nc.vector.tensor_copy(picked[:], tab_s[:].indirect(offsets[:, a * LIST_COLS : (a + 1) * LIST_COLS]))
+            ordered = keep.tile([P, PASS], U8, name=f"v_s{a}", align_bytes=64)
+            nc.vector.tensor_copy(
+                ordered[:].rearrange("p (t c i) -> p c t i", t=PACK, i=16),
+                picked[:].rearrange("p (c i t) -> p c t i", t=PACK, i=16),
+            )
+            return ordered
+
+        def gather_words(a):
+            picked = ring.tile([P, PASS], U32, name="picked_w", bufs=2, align_bytes=64)
+            nc.vector.tensor_copy(
+                picked[:], tab_w[:].bitcast(U32).indirect(offsets[:, a * LIST_COLS : (a + 1) * LIST_COLS])
+            )
+            ordered = keep.tile([P, PASS], U32, name=f"v_w{a}", align_bytes=64)
+            nc.vector.tensor_copy(
+                ordered[:].rearrange("p (t c i) -> p c t i", t=PACK, i=4),
+                picked[:].rearrange("p (c i t) -> p c t i", t=PACK, i=4),
+            )
+            return ordered
+
+        def quantise_x(mt):
+            grouped = keep.tile([P, M_TILE * PACK], BF16, name=f"x_bf{mt}", align_bytes=64)
+            nc.scalar.copy(
+                grouped[:].rearrange("p (c i t) -> p c t i", t=PACK, i=4),
+                x_raw[mt][:].rearrange("p t (c i) -> p c t i", i=4),
+            )
+            codes = keep.tile([P, M_TILE], U32, name=f"x_w{mt}", align_bytes=64)
+            scales = keep.tile([P, M_TILE], U8, name=f"x_s{mt}", align_bytes=64)
+            nc.vector.quantize_mx(codes[:].bitcast(FP8X4), scales[:], grouped[:])
+            return codes, scales
+
+        v_s = [gather_scales(a) for a in range(J_PASSES)]
+        x_q = [quantise_x(0)]
+        v_w = [gather_words(0)]
+        v_w.extend(gather_words(a) for a in range(1, J_PASSES))
+        x_q.append(quantise_x(1))
+
+        y = [[psum.tile([P, M_TILE], F32, name=f"y{mt}{u}") for u in range(N_TILES)] for mt in range(M_TILES)]
+
+        def first_stage(mt, a):
+            planes = ring.tile([P, PACK, M_TILE], BF16, name="h_planes", bufs=8, align_bytes=64)
+            for t in range(PACK):
+                d = psum.tile([P, M_TILE], F32, name=f"d{t}")
+                cols = slice(t * P, (t + 1) * P)
+                nc.tensor.matmul_mx(
+                    d[:],
+                    lhsT=v_w[a][:, cols].bitcast(FP8X4),
+                    lhsT_scale=v_s[a][:, cols],
+                    rhs=x_q[mt][0][:].bitcast(FP8X4),
+                    rhs_scale=x_q[mt][1][:],
+                    start=True,
+                    stop=True,
+                )
+                c, u = divmod(a * PACK + t, N_TILES)
+                nc.scalar.activation(planes[:, t, :], d[:], ACT.Exp, bias=results[0][:, u, c : c + 1])
+            return planes
+
+        def weigh(a, planes):
+            weighed = ring.tile([P, PACK, M_TILE], BF16, name="h_weighed", bufs=2, align_bytes=64)
+            for t in range(PACK):
+                col = slice(a * PACK + t, a * PACK + t + 1)
+                nc.vector.tensor_scalar(weighed[:, t, :], planes[:, t, :], power[:, col], None, ALU.mult)
+            return weighed
+
+        def interleave(weighed):
+            grouped = ring.tile([P, M_TILE * PACK], BF16, name="h_grouped", bufs=2, align_bytes=64)
+            nc.vector.tensor_copy(
+                grouped[:].rearrange("p (c i t) -> p c t i", t=PACK, i=4),
+                weighed[:].rearrange("p t (c i) -> p c t i", i=4),
+            )
+            return grouped
+
+        def second_stage(mt, a, grouped):
+            codes = ring.tile([P, M_TILE], U32, name="h_w", bufs=3, align_bytes=64)
+            scales = ring.tile([P, M_TILE], U8, name="h_s", bufs=3, align_bytes=64)
+            nc.vector.quantize_mx(codes[:].bitcast(FP8X4), scales[:], grouped[:])
+            for u in range(N_TILES):
+                cols = slice(u * P, (u + 1) * P)
+                nc.tensor.matmul_mx(
+                    y[mt][u][:],
+                    lhsT=al4_w[:, a, u * P // 2 : (u + 1) * P // 2].bitcast(U8).bitcast(FP4X4),
+                    lhsT_scale=al4_s[:, a, cols],
+                    rhs=codes[:].bitcast(FP8X4),
+                    rhs_scale=scales[:],
+                    start=(a == 0),
+                    stop=False,
+                )
+                nc.tensor.matmul_mx(
+                    y[mt][u][:],
+                    lhsT=al8_w[:, a, cols].bitcast(FP8X4),
+                    lhsT_scale=al8_s[:, a, cols],
+                    rhs=codes[:].bitcast(FP8X4),
+                    rhs_scale=scales[:],
+                    start=False,
+                    stop=(a == J_PASSES - 1),
+                )
+
+        steps = [(mt, a) for mt in range(M_TILES) for a in range(J_PASSES)]
+        grouped_prev = None
+        for s, (mt, a) in enumerate(steps):
+            planes = first_stage(mt, a)
+            weighed = weigh(a, planes)
+            if grouped_prev is not None:
+                second_stage(*steps[s - 1], grouped_prev)
+            grouped_prev = interleave(weighed)
+        second_stage(*steps[-1], grouped_prev)
+
+        for mt in range(M_TILES):
+            for u in range(N_TILES):
+                result = results[mt][:, u, :]
+                nc.scalar.activation(result, y[mt][u][:], ACT.Gelu_apprx_tanh, bias=b_t[:, u : u + 1])
+                nc.sync.dma_start(out[u * P : (u + 1) * P, mt * M_TILE : (mt + 1) * M_TILE], result)

@@ -22,6 +22,7 @@ PASS = P * PACK
 J_PASSES = J // PASS
 M_TILE = 512
 M_TILES = M // M_TILE
+HALF = M_TILE // 2
 N_TILES = N // P
 LIST_COLS = PASS // 16
 
@@ -59,6 +60,7 @@ def tile_list_kernl_exp_res_gelu_kernel(
         tab_w = keep.tile([P, T], I32, name="tab_w", align_bytes=64)
         nc.sync.dma_start(x_raw[0][:], x_view[:, :, 0:M_TILE])
         nc.sync.dma_start(tab_w[:], tab_words[0].rearrange("p t i -> p (t i)").bitcast(I32))
+        nc.sync.dma_start(x_raw[1][:], x_view[:, :, M_TILE:M])
 
         al4_s = keep.tile([P, J_PASSES, N], U8, name="al4_s", align_bytes=64)
         al8_s = keep.tile([P, J_PASSES, N], U8, name="al8_s", align_bytes=64)
@@ -74,7 +76,6 @@ def tile_list_kernl_exp_res_gelu_kernel(
                     plane[32 * q : 32 * q + 4, :, :].bitcast(I32),
                     rows[:, 4 * q : 4 * q + 4, :].rearrange("a r n -> r a n").bitcast(I32),
                 )
-        nc.sync.dma_start(x_raw[1][:], x_view[:, :, M_TILE:M])
         b_t = keep.tile([P, N_TILES], F32, name="b_t")
         with nc.allow_non_contiguous_dma(reason="one bias value a partition"):
             nc.sync.dma_start(b_t[:], b.rearrange("(u p) -> p u", p=P))
@@ -84,14 +85,16 @@ def tile_list_kernl_exp_res_gelu_kernel(
         mant = keep.tile([P, J_PASSES * PACK], F32, name="mant")
         nc.vector.tensor_scalar(mant[:].bitcast(I32), cw_bits, MANTISSA, ONE_BITS, ALU.bitwise_and, ALU.bitwise_or)
         nc.vector.tensor_scalar(power[:].bitcast(I32), cw_bits, SIGN_AND_EXPONENT, None, ALU.bitwise_and)
+        power_bf = keep.tile([P, J_PASSES * PACK], BF16, name="power_bf")
+        nc.vector.tensor_copy(power_bf[:], power[:])
         log_mant = keep.tile([P, J_PASSES * PACK], F32, name="log_mant")
         nc.scalar.activation(log_mant[:], mant[:], ACT.Ln)
-        results = [keep.tile([P, N_TILES, M_TILE], F32, name=f"result{mt}") for mt in range(M_TILES)]
-        shift = results[0][:, :, 0 : J_PASSES * PACK // N_TILES].rearrange("p u c -> p c u")
+        results = [keep.tile([P, 2, N_TILES, HALF], F32, name=f"result{mt}") for mt in range(M_TILES)]
+        shift = results[0][:].rearrange("p h u m -> p (h u) m")[:, :, 0:J_PASSES]
         nc.vector.tensor_tensor(
-            shift,
-            log_mant[:].rearrange("p (c u) -> p c u", u=N_TILES),
-            cb_t[:].rearrange("p a (c u) -> p (a c) u", u=N_TILES),
+            shift.rearrange("p t a -> p a t"),
+            log_mant[:].rearrange("p (a t) -> p a t", t=PACK),
+            cb_t[:],
             ALU.subtract,
         )
 
@@ -106,14 +109,10 @@ def tile_list_kernl_exp_res_gelu_kernel(
             return ordered
 
         def gather_words(a):
-            picked = ring.tile([P, PASS], U32, name="picked_w", bufs=2, align_bytes=64)
-            nc.vector.tensor_copy(
-                picked[:], tab_w[:].bitcast(U32).indirect(offsets[:, a * LIST_COLS : (a + 1) * LIST_COLS])
-            )
             ordered = keep.tile([P, PASS], U32, name=f"v_w{a}", align_bytes=64)
             nc.vector.tensor_copy(
-                ordered[:].rearrange("p (t c i) -> p c t i", t=PACK, i=4),
-                picked[:].rearrange("p (c i t) -> p c t i", t=PACK, i=4),
+                ordered[:].rearrange("p (t q) -> p q t", t=PACK),
+                tab_w[:].bitcast(U32).indirect(offsets[:, a * LIST_COLS : (a + 1) * LIST_COLS]),
             )
             return ordered
 
@@ -134,7 +133,7 @@ def tile_list_kernl_exp_res_gelu_kernel(
         v_w.extend(gather_words(a) for a in range(1, J_PASSES))
         x_q.append(quantise_x(1))
 
-        y = [[psum.tile([P, M_TILE], F32, name=f"y{mt}{u}") for u in range(N_TILES)] for mt in range(M_TILES)]
+        y = [[psum.tile([P, N_TILES, HALF], F32, name=f"y{mt}{h}") for h in range(2)] for mt in range(M_TILES)]
 
         def first_stage(mt, a):
             planes = ring.tile([P, PACK, M_TILE], BF16, name="h_planes", bufs=8, align_bytes=64)
@@ -150,49 +149,53 @@ def tile_list_kernl_exp_res_gelu_kernel(
                     start=True,
                     stop=True,
                 )
-                c, u = divmod(a * PACK + t, N_TILES)
-                nc.scalar.activation(planes[:, t, :], d[:], ACT.Exp, bias=results[0][:, u, c : c + 1])
+                nc.scalar.activation(planes[:, t, :], d[:], ACT.Exp, bias=shift[:, t, a : a + 1])
             return planes
 
         def weigh(a, planes):
             weighed = ring.tile([P, PACK, M_TILE], BF16, name="h_weighed", bufs=2, align_bytes=64)
             for t in range(PACK):
                 col = slice(a * PACK + t, a * PACK + t + 1)
-                nc.vector.tensor_scalar(weighed[:, t, :], planes[:, t, :], power[:, col], None, ALU.mult)
+                nc.vector.tensor_scalar(weighed[:, t, :], planes[:, t, :], power_bf[:, col], None, ALU.mult)
             return weighed
 
-        def interleave(weighed):
+        def interleave(weighed, lo, width):
             grouped = ring.tile([P, M_TILE * PACK], BF16, name="h_grouped", bufs=2, align_bytes=64)
             nc.vector.tensor_copy(
-                grouped[:].rearrange("p (c i t) -> p c t i", t=PACK, i=4),
-                weighed[:].rearrange("p t (c i) -> p c t i", i=4),
+                grouped[:, 0 : width * PACK].rearrange("p (c i t) -> p c t i", t=PACK, i=4),
+                weighed[:, :, lo : lo + width].rearrange("p t (c i) -> p c t i", i=4),
             )
             return grouped
 
-        def second_stage(mt, a, grouped):
-            codes = ring.tile([P, M_TILE], U32, name="h_w", bufs=3, align_bytes=64)
-            scales = ring.tile([P, M_TILE], U8, name="h_s", bufs=3, align_bytes=64)
-            nc.vector.quantize_mx(codes[:].bitcast(FP8X4), scales[:], grouped[:])
-            for u in range(N_TILES):
-                cols = slice(u * P, (u + 1) * P)
-                nc.tensor.matmul_mx(
-                    y[mt][u][:],
-                    lhsT=al4_w[:, a, u * P // 2 : (u + 1) * P // 2].bitcast(U8).bitcast(FP4X4),
-                    lhsT_scale=al4_s[:, a, cols],
-                    rhs=codes[:].bitcast(FP8X4),
-                    rhs_scale=scales[:],
-                    start=(a == 0),
-                    stop=False,
-                )
-                nc.tensor.matmul_mx(
-                    y[mt][u][:],
-                    lhsT=al8_w[:, a, cols].bitcast(FP8X4),
-                    lhsT_scale=al8_s[:, a, cols],
-                    rhs=codes[:].bitcast(FP8X4),
-                    rhs_scale=scales[:],
-                    start=False,
-                    stop=(a == J_PASSES - 1),
-                )
+        def second_stage(mt, a, grouped, lo, width):
+            codes = ring.tile([P, M_TILE], U32, name="h_w", bufs=4, align_bytes=64)
+            scales = ring.tile([P, M_TILE], U8, name="h_s", bufs=4, align_bytes=64)
+            nc.vector.quantize_mx(codes[:, 0:width].bitcast(FP8X4), scales[:, 0:width], grouped[:, 0 : width * PACK])
+            for half in range(lo // HALF, (lo + width) // HALF):
+                bank = y[mt][half]
+                for u in range(N_TILES):
+                    cols = slice(u * P, (u + 1) * P)
+                    for c in range(HALF // P):
+                        src = slice(half * HALF - lo + c * P, half * HALF - lo + (c + 1) * P)
+                        nc.tensor.matmul_mx(
+                            bank[:, u, c * P : (c + 1) * P],
+                            lhsT=al4_w[:, a, u * P // 2 : (u + 1) * P // 2].bitcast(U8).bitcast(FP4X4),
+                            lhsT_scale=al4_s[:, a, cols],
+                            rhs=codes[:, src].bitcast(FP8X4),
+                            rhs_scale=scales[:, src],
+                            start=(a == 0 and u == 0 and c == 0),
+                            stop=False,
+                        )
+                    src = slice(half * HALF - lo, (half + 1) * HALF - lo)
+                    nc.tensor.matmul_mx(
+                        bank[:, u, :],
+                        lhsT=al8_w[:, a, cols].bitcast(FP8X4),
+                        lhsT_scale=al8_s[:, a, cols],
+                        rhs=codes[:, src].bitcast(FP8X4),
+                        rhs_scale=scales[:, src],
+                        start=False,
+                        stop=(a == J_PASSES - 1 and u == N_TILES - 1),
+                    )
 
         steps = [(mt, a) for mt in range(M_TILES) for a in range(J_PASSES)]
         grouped_prev = None
@@ -200,12 +203,19 @@ def tile_list_kernl_exp_res_gelu_kernel(
             planes = first_stage(mt, a)
             weighed = weigh(a, planes)
             if grouped_prev is not None:
-                second_stage(*steps[s - 1], grouped_prev)
-            grouped_prev = interleave(weighed)
-        second_stage(*steps[-1], grouped_prev)
+                second_stage(*steps[s - 1], grouped_prev, 0, M_TILE)
+            if s + 1 < len(steps):
+                grouped_prev = interleave(weighed, 0, M_TILE)
+        halves = [interleave(weighed, half * HALF, HALF) for half in range(2)]
+        for half in range(2):
+            second_stage(*steps[-1], halves[half], half * HALF, HALF)
 
+        out_view = out.rearrange("(u p) m -> p u m", p=P)
         for mt in range(M_TILES):
-            for u in range(N_TILES):
-                result = results[mt][:, u, :]
-                nc.scalar.activation(result, y[mt][u][:], ACT.Gelu_apprx_tanh, bias=b_t[:, u : u + 1])
-                nc.sync.dma_start(out[u * P : (u + 1) * P, mt * M_TILE : (mt + 1) * M_TILE], result)
+            for half in range(2):
+                for u in range(N_TILES):
+                    nc.scalar.activation(
+                        results[mt][:, half, u, :], y[mt][half][:, u, :], ACT.Gelu_apprx_tanh, bias=b_t[:, u : u + 1]
+                    )
+                lo = mt * M_TILE + half * HALF
+                nc.sync.dma_start(out_view[:, :, lo : lo + HALF], results[mt][:, half, :, :])

@@ -89,14 +89,29 @@ def tile_list_kernl_exp_res_gelu_kernel(
         nc.vector.tensor_copy(power_bf[:], power[:])
         log_mant = keep.tile([P, J_PASSES * PACK], F32, name="log_mant")
         nc.scalar.activation(log_mant[:], mant[:], ACT.Ln)
-        results = [keep.tile([P, 2, N_TILES, HALF], F32, name=f"result{mt}") for mt in range(M_TILES)]
-        shift = results[0][:].rearrange("p h u m -> p (h u) m")[:, :, 0:J_PASSES]
+        result_first = keep.tile([P, N_TILES, M_TILE], F32, name="result_first")
+        result_last = keep.tile([P, 2, N_TILES, HALF], F32, name="result_last")
+        shift = result_first[:, :, 0 : 2 * J_PASSES].rearrange("p u (a e) -> p a u e", e=2)
         nc.vector.tensor_tensor(
-            shift.rearrange("p t a -> p a t"),
-            log_mant[:].rearrange("p (a t) -> p a t", t=PACK),
-            cb_t[:],
+            shift,
+            log_mant[:].rearrange("p (a u e) -> p a u e", u=2, e=2),
+            cb_t[:].rearrange("p a (u e) -> p a u e", e=2),
             ALU.subtract,
         )
+        steps = [(mt, a) for mt in range(M_TILES) for a in range(J_PASSES)]
+        own_shift = {}
+        for s in range(1, len(steps)):
+            a = steps[s][1]
+            for tag, t in (("grouped", 1), ("codes", 3 if s + 1 < len(steps) else 2)):
+                column = keep.tile([P, 1], F32, name=f"shift{s}{t}", tag=f"{tag}{s - 1}", align_bytes=64)
+                nc.scalar.activation(
+                    column[:],
+                    cb_t[:, a, t : t + 1],
+                    ACT.Identity,
+                    bias=log_mant[:, a * PACK + t : a * PACK + t + 1],
+                    scale=-1.0,
+                )
+                own_shift[s, t] = column[:]
 
         def gather_scales(a):
             picked = ring.tile([P, PASS], U8, name="picked_s", bufs=2, align_bytes=64)
@@ -118,10 +133,16 @@ def tile_list_kernl_exp_res_gelu_kernel(
 
         def quantise_x(mt):
             grouped = keep.tile([P, M_TILE * PACK], BF16, name=f"x_bf{mt}", align_bytes=64)
+            split = M_TILE if mt == 0 else HALF
             nc.scalar.copy(
-                grouped[:].rearrange("p (c i t) -> p c t i", t=PACK, i=4),
-                x_raw[mt][:].rearrange("p t (c i) -> p c t i", i=4),
+                grouped[:, 0 : split * PACK].rearrange("p (c i t) -> p c t i", t=PACK, i=4),
+                x_raw[mt][:, :, 0:split].rearrange("p t (c i) -> p c t i", i=4),
             )
+            if split < M_TILE:
+                nc.vector.tensor_copy(
+                    grouped[:, split * PACK :].rearrange("p (c i t) -> p c t i", t=PACK, i=4),
+                    x_raw[mt][:, :, split:].rearrange("p t (c i) -> p c t i", i=4),
+                )
             codes = keep.tile([P, M_TILE], U32, name=f"x_w{mt}", align_bytes=64)
             scales = keep.tile([P, M_TILE], U8, name=f"x_s{mt}", align_bytes=64)
             nc.vector.quantize_mx(codes[:].bitcast(FP8X4), scales[:], grouped[:])
@@ -133,10 +154,12 @@ def tile_list_kernl_exp_res_gelu_kernel(
         v_w.extend(gather_words(a) for a in range(1, J_PASSES))
         x_q.append(quantise_x(1))
 
-        y = [[psum.tile([P, N_TILES, HALF], F32, name=f"y{mt}{h}") for h in range(2)] for mt in range(M_TILES)]
+        y_first = [psum.tile([P, M_TILE], F32, name=f"y_first{u}") for u in range(N_TILES)]
+        y_last = [psum.tile([P, N_TILES, HALF], F32, name=f"y_last{h}") for h in range(2)]
 
-        def first_stage(mt, a):
-            planes = ring.tile([P, PACK, M_TILE], BF16, name="h_planes", bufs=8, align_bytes=64)
+        def first_stage(s):
+            mt, a = steps[s]
+            planes = ring.tile([P, PACK, M_TILE], BF16, name="h_planes", bufs=6, align_bytes=64)
             for t in range(PACK):
                 d = psum.tile([P, M_TILE], F32, name=f"d{t}")
                 cols = slice(t * P, (t + 1) * P)
@@ -149,73 +172,81 @@ def tile_list_kernl_exp_res_gelu_kernel(
                     start=True,
                     stop=True,
                 )
-                nc.scalar.activation(planes[:, t, :], d[:], ACT.Exp, bias=shift[:, t, a : a + 1])
+                bias = own_shift.get((s, t), shift[:, a, t // 2, t % 2 : t % 2 + 1])
+                nc.scalar.activation(planes[:, t, :], d[:], ACT.Exp, bias=bias)
             return planes
 
-        def weigh(a, planes):
-            weighed = ring.tile([P, PACK, M_TILE], BF16, name="h_weighed", bufs=2, align_bytes=64)
-            for t in range(PACK):
-                col = slice(a * PACK + t, a * PACK + t + 1)
-                nc.vector.tensor_scalar(weighed[:, t, :], planes[:, t, :], power_bf[:, col], None, ALU.mult)
-            return weighed
+        def weigh(s, t, planes, weighed):
+            col = steps[s][1] * PACK + t
+            nc.vector.tensor_scalar(weighed[:, t, :], planes[:, t, :], power_bf[:, col : col + 1], None, ALU.mult)
 
-        def interleave(weighed, lo, width):
-            grouped = ring.tile([P, M_TILE * PACK], BF16, name="h_grouped", bufs=2, align_bytes=64)
+        def interleave(weighed, lo, width, tag):
+            grouped = keep.tile([P, width * PACK], BF16, name="grouped", tag=f"grouped{tag}", align_bytes=64)
             nc.vector.tensor_copy(
-                grouped[:, 0 : width * PACK].rearrange("p (c i t) -> p c t i", t=PACK, i=4),
+                grouped[:].rearrange("p (c i t) -> p c t i", t=PACK, i=4),
                 weighed[:, :, lo : lo + width].rearrange("p t (c i) -> p c t i", i=4),
             )
             return grouped
 
-        def second_stage(mt, a, grouped, lo, width):
-            codes = ring.tile([P, M_TILE], U32, name="h_w", bufs=4, align_bytes=64)
-            scales = ring.tile([P, M_TILE], U8, name="h_s", bufs=4, align_bytes=64)
-            nc.vector.quantize_mx(codes[:, 0:width].bitcast(FP8X4), scales[:, 0:width], grouped[:, 0 : width * PACK])
-            for half in range(lo // HALF, (lo + width) // HALF):
-                bank = y[mt][half]
-                for u in range(N_TILES):
-                    cols = slice(u * P, (u + 1) * P)
-                    for c in range(HALF // P):
-                        src = slice(half * HALF - lo + c * P, half * HALF - lo + (c + 1) * P)
-                        nc.tensor.matmul_mx(
-                            bank[:, u, c * P : (c + 1) * P],
-                            lhsT=al4_w[:, a, u * P // 2 : (u + 1) * P // 2].bitcast(U8).bitcast(FP4X4),
-                            lhsT_scale=al4_s[:, a, cols],
-                            rhs=codes[:, src].bitcast(FP8X4),
-                            rhs_scale=scales[:, src],
-                            start=(a == 0 and u == 0 and c == 0),
-                            stop=False,
-                        )
-                    src = slice(half * HALF - lo, (half + 1) * HALF - lo)
-                    nc.tensor.matmul_mx(
-                        bank[:, u, :],
-                        lhsT=al8_w[:, a, cols].bitcast(FP8X4),
-                        lhsT_scale=al8_s[:, a, cols],
-                        rhs=codes[:, src].bitcast(FP8X4),
-                        rhs_scale=scales[:, src],
-                        start=False,
-                        stop=(a == J_PASSES - 1 and u == N_TILES - 1),
-                    )
+        def product(target, a, u, codes, scales, fp4, start, stop):
+            cols = slice(u * P, (u + 1) * P)
+            if fp4:
+                lhs, lhs_s = al4_w[:, a, u * P // 2 : (u + 1) * P // 2].bitcast(U8).bitcast(FP4X4), al4_s[:, a, cols]
+            else:
+                lhs, lhs_s = al8_w[:, a, cols].bitcast(FP8X4), al8_s[:, a, cols]
+            nc.tensor.matmul_mx(
+                target, lhsT=lhs, lhsT_scale=lhs_s, rhs=codes.bitcast(FP8X4), rhs_scale=scales, start=start, stop=stop
+            )
 
-        steps = [(mt, a) for mt in range(M_TILES) for a in range(J_PASSES)]
-        grouped_prev = None
-        for s, (mt, a) in enumerate(steps):
-            planes = first_stage(mt, a)
-            weighed = weigh(a, planes)
-            if grouped_prev is not None:
-                second_stage(*steps[s - 1], grouped_prev, 0, M_TILE)
+        def second_stage(s, grouped, lo, width, tag):
+            mt, a = steps[s]
+            first, last = a == 0, a == J_PASSES - 1
+            codes = keep.tile([P, width], U32, name="h_w", tag=f"codes{tag}", align_bytes=64)
+            scales = ring.tile([P, M_TILE], U8, name="h_s", bufs=4, align_bytes=64)
+            nc.vector.quantize_mx(codes[:].bitcast(FP8X4), scales[:, 0:width], grouped[:])
+            if mt == 0:
+                for u in range(N_TILES):
+                    product(y_first[u][:], a, u, codes[:], scales[:], True, first, False)
+                    product(y_first[u][:], a, u, codes[:], scales[:], False, False, last)
+                return
+            for half in range(lo // HALF, (lo + width) // HALF):
+                base = half * HALF - lo
+                for u in range(N_TILES):
+                    for c in range(HALF // P):
+                        src = slice(base + c * P, base + (c + 1) * P)
+                        target = y_last[half][:, u, c * P : (c + 1) * P]
+                        product(target, a, u, codes[:, src], scales[:, src], True, first and u == 0 and c == 0, False)
+                    src = slice(base, base + HALF)
+                    closes = last and u == N_TILES - 1
+                    product(y_last[half][:, u, :], a, u, codes[:, src], scales[:, src], False, False, closes)
+
+        weighed_prev = None
+        for s in range(len(steps)):
+            planes = first_stage(s)
+            weighed = ring.tile([P, PACK, M_TILE], BF16, name="h_weighed", bufs=3, align_bytes=64)
+            weigh(s, 0, planes, weighed)
+            weigh(s, 1, planes, weighed)
+            if s > 0:
+                grouped = interleave(weighed_prev, 0, M_TILE, s - 1)
+            weigh(s, 2, planes, weighed)
             if s + 1 < len(steps):
-                grouped_prev = interleave(weighed, 0, M_TILE)
-        halves = [interleave(weighed, half * HALF, HALF) for half in range(2)]
+                weigh(s, 3, planes, weighed)
+            if s > 0:
+                second_stage(s - 1, grouped, 0, M_TILE, s - 1)
+            weighed_prev = weighed
+        weigh(len(steps) - 1, 3, planes, weighed)
+        halves = [interleave(weighed, half * HALF, HALF, f"last{half}") for half in range(2)]
         for half in range(2):
-            second_stage(*steps[-1], halves[half], half * HALF, HALF)
+            second_stage(len(steps) - 1, halves[half], half * HALF, HALF, f"last{half}")
 
         out_view = out.rearrange("(u p) m -> p u m", p=P)
-        for mt in range(M_TILES):
-            for half in range(2):
-                for u in range(N_TILES):
-                    nc.scalar.activation(
-                        results[mt][:, half, u, :], y[mt][half][:, u, :], ACT.Gelu_apprx_tanh, bias=b_t[:, u : u + 1]
-                    )
-                lo = mt * M_TILE + half * HALF
-                nc.sync.dma_start(out_view[:, :, lo : lo + HALF], results[mt][:, half, :, :])
+        for u in range(N_TILES):
+            nc.scalar.activation(result_first[:, u, :], y_first[u][:], ACT.Gelu_apprx_tanh, bias=b_t[:, u : u + 1])
+        nc.sync.dma_start(out_view[:, :, 0:M_TILE], result_first[:])
+        for half in range(2):
+            for u in range(N_TILES):
+                nc.scalar.activation(
+                    result_last[:, half, u, :], y_last[half][:, u, :], ACT.Gelu_apprx_tanh, bias=b_t[:, u : u + 1]
+                )
+            lo = M_TILE + half * HALF
+            nc.sync.dma_start(out_view[:, :, lo : lo + HALF], result_last[:, half, :, :])

@@ -45,8 +45,8 @@ def tile_list_kernl_exp_res_gelu_kernel(
 
         tab_s = keep.tile([P, T], U8, name="tab_s", align_bytes=64)
         nc.vector.memset(tab_s[:].bitcast(I32), 0)
-        for q in range(4):
-            nc.sync.dma_start(
+        for q, queue in ((0, nc.sync), (2, nc.scalar), (1, nc.sync), (3, nc.scalar)):
+            queue.dma_start(
                 tab_s[32 * q : 32 * q + 4, :].bitcast(I32), tab_scales[0, 4 * q : 4 * q + 4, :].bitcast(I32)
             )
 
@@ -71,7 +71,7 @@ def tile_list_kernl_exp_res_gelu_kernel(
         nc.sync.dma_start(al8_w[:], al8_words.rearrange("a p n i -> p a (n i)").bitcast(I32))
         nc.sync.dma_start(al4_w[:], al4_words.rearrange("a p c -> p a c").bitcast(I32))
         for plane, rows in ((al4_s, al4_scales), (al8_s, al8_scales)):
-            for q in range(4):
+            for q in (0, 2, 1, 3):
                 nc.sync.dma_start(
                     plane[32 * q : 32 * q + 4, :, :].bitcast(I32),
                     rows[:, 4 * q : 4 * q + 4, :].rearrange("a r n -> r a n").bitcast(I32),
@@ -91,18 +91,14 @@ def tile_list_kernl_exp_res_gelu_kernel(
         nc.scalar.activation(log_mant[:], mant[:], ACT.Ln)
         result_first = keep.tile([P, N_TILES, M_TILE], F32, name="result_first")
         result_last = keep.tile([P, 2, N_TILES, HALF], F32, name="result_last")
-        shift = result_first[:, :, 0 : 2 * J_PASSES].rearrange("p u (a e) -> p a u e", e=2)
-        nc.vector.tensor_tensor(
-            shift,
-            log_mant[:].rearrange("p (a u e) -> p a u e", u=2, e=2),
-            cb_t[:].rearrange("p a (u e) -> p a u e", e=2),
-            ALU.subtract,
-        )
+        shift = keep.tile([P, J_PASSES * PACK], F32, name="shift")
+        nc.vector.tensor_tensor(shift[:], log_mant[:], cb_t[:].rearrange("p a t -> p (a t)"), ALU.subtract)
         steps = [(mt, a) for mt in range(M_TILES) for a in range(J_PASSES)]
         own_shift = {}
         for s in range(1, len(steps)):
             a = steps[s][1]
-            for tag, t in (("grouped", 1), ("codes", 3 if s + 1 < len(steps) else 2)):
+            holds = (("grouped", 1), ("codes", 3)) if s + 1 < len(steps) else (("grouped", 1), ("codes", 2), ("b", 3))
+            for tag, t in holds:
                 column = keep.tile([P, 1], F32, name=f"shift{s}{t}", tag=f"{tag}{s - 1}", align_bytes=64)
                 nc.scalar.activation(
                     column[:],
@@ -114,14 +110,14 @@ def tile_list_kernl_exp_res_gelu_kernel(
                 own_shift[s, t] = column[:]
 
         def gather_scales(a):
-            picked = ring.tile([P, PASS], U8, name="picked_s", bufs=2, align_bytes=64)
-            nc.vector.tensor_copy(picked[:], tab_s[:].indirect(offsets[:, a * LIST_COLS : (a + 1) * LIST_COLS]))
-            ordered = keep.tile([P, PASS], U8, name=f"v_s{a}", align_bytes=64)
+            picked = keep.tile([P, 2 * PASS], U8, name=f"picked_s{a}", align_bytes=64)
+            nc.vector.tensor_copy(picked[:], tab_s[:].indirect(offsets[:, a * LIST_COLS : (a + 2) * LIST_COLS]))
+            ordered = keep.tile([P, 2 * PASS], U8, name=f"v_s{a}", align_bytes=64)
             nc.vector.tensor_copy(
-                ordered[:].rearrange("p (t c i) -> p c t i", t=PACK, i=16),
-                picked[:].rearrange("p (c i t) -> p c t i", t=PACK, i=16),
+                ordered[:].rearrange("p (a t c i) -> p a c t i", a=2, t=PACK, i=16),
+                picked[:].rearrange("p (a c i t) -> p a c t i", a=2, t=PACK, i=16),
             )
-            return ordered
+            return [ordered[:, 0:PASS], ordered[:, PASS:]]
 
         def gather_words(a):
             ordered = keep.tile([P, PASS], U32, name=f"v_w{a}", align_bytes=64)
@@ -133,22 +129,20 @@ def tile_list_kernl_exp_res_gelu_kernel(
 
         def quantise_x(mt):
             grouped = keep.tile([P, M_TILE * PACK], BF16, name=f"x_bf{mt}", align_bytes=64)
-            split = M_TILE if mt == 0 else HALF
-            nc.scalar.copy(
-                grouped[:, 0 : split * PACK].rearrange("p (c i t) -> p c t i", t=PACK, i=4),
-                x_raw[mt][:, :, 0:split].rearrange("p t (c i) -> p c t i", i=4),
-            )
-            if split < M_TILE:
-                nc.vector.tensor_copy(
-                    grouped[:, split * PACK :].rearrange("p (c i t) -> p c t i", t=PACK, i=4),
-                    x_raw[mt][:, :, split:].rearrange("p t (c i) -> p c t i", i=4),
+            shares = [(nc.scalar.copy, 0, M_TILE)]
+            if mt == 1:
+                shares = [(nc.scalar.copy, 0, HALF), (nc.vector.tensor_copy, HALF, M_TILE)]
+            for copy, lo, hi in shares:
+                copy(
+                    grouped[:, lo * PACK : hi * PACK].rearrange("p (c i t) -> p c t i", t=PACK, i=4),
+                    x_raw[mt][:, :, lo:hi].rearrange("p t (c i) -> p c t i", i=4),
                 )
             codes = keep.tile([P, M_TILE], U32, name=f"x_w{mt}", align_bytes=64)
             scales = keep.tile([P, M_TILE], U8, name=f"x_s{mt}", align_bytes=64)
             nc.vector.quantize_mx(codes[:].bitcast(FP8X4), scales[:], grouped[:])
             return codes, scales
 
-        v_s = [gather_scales(a) for a in range(J_PASSES)]
+        v_s = gather_scales(0) + gather_scales(2)
         x_q = [quantise_x(0)]
         v_w = [gather_words(0)]
         v_w.extend(gather_words(a) for a in range(1, J_PASSES))
@@ -172,7 +166,7 @@ def tile_list_kernl_exp_res_gelu_kernel(
                     start=True,
                     stop=True,
                 )
-                bias = own_shift.get((s, t), shift[:, a, t // 2, t % 2 : t % 2 + 1])
+                bias = own_shift.get((s, t), shift[:, a * PACK + t : a * PACK + t + 1])
                 nc.scalar.activation(planes[:, t, :], d[:], ACT.Exp, bias=bias)
             return planes
 
@@ -239,14 +233,16 @@ def tile_list_kernl_exp_res_gelu_kernel(
         for half in range(2):
             second_stage(len(steps) - 1, halves[half], half * HALF, HALF, f"last{half}")
 
+        b_late = keep.tile([P, N_TILES], F32, name="b_late", tag=f"b{len(steps) - 2}", align_bytes=64)
+        nc.scalar.copy(b_late[:], b_t[:])
         out_view = out.rearrange("(u p) m -> p u m", p=P)
         for u in range(N_TILES):
-            nc.scalar.activation(result_first[:, u, :], y_first[u][:], ACT.Gelu_apprx_tanh, bias=b_t[:, u : u + 1])
+            nc.scalar.activation(result_first[:, u, :], y_first[u][:], ACT.Gelu_apprx_tanh, bias=b_late[:, u : u + 1])
         nc.sync.dma_start(out_view[:, :, 0:M_TILE], result_first[:])
         for half in range(2):
             for u in range(N_TILES):
                 nc.scalar.activation(
-                    result_last[:, half, u, :], y_last[half][:, u, :], ACT.Gelu_apprx_tanh, bias=b_t[:, u : u + 1]
+                    result_last[:, half, u, :], y_last[half][:, u, :], ACT.Gelu_apprx_tanh, bias=b_late[:, u : u + 1]
                 )
-            lo = M_TILE + half * HALF
-            nc.sync.dma_start(out_view[:, :, lo : lo + HALF], result_last[:, half, :, :])
+                lo = M_TILE + half * HALF
+                nc.sync.dma_start(out_view[:, u, lo : lo + HALF], result_last[:, half, u, :])

@@ -45,8 +45,8 @@ def tile_list_kernl_exp_res_gelu_kernel(
 
         tab_s = keep.tile([P, T], U8, name="tab_s", align_bytes=64)
         nc.vector.memset(tab_s[:].bitcast(I32), 0)
-        for q, queue in ((0, nc.sync), (2, nc.scalar), (1, nc.sync), (3, nc.scalar)):
-            queue.dma_start(
+        for q in (0, 2, 1, 3):
+            nc.sync.dma_start(
                 tab_s[32 * q : 32 * q + 4, :].bitcast(I32), tab_scales[0, 4 * q : 4 * q + 4, :].bitcast(I32)
             )
 

from contextlib import ExitStack

import concourse.mybir as mybir

K, M, N, J, T = 512, 1024, 256, 2048, 4096
FLOPS = 2 * K * J * M + 2 * 2 * J * N * M

F32 = mybir.dt.float32
BF16 = mybir.dt.bfloat16
I32 = mybir.dt.int32
U32 = mybir.dt.uint32
U16 = mybir.dt.uint16
U8 = mybir.dt.uint8
FP8X4 = mybir.dt.float8_e4m3fn_x4
FP4X4 = mybir.dt.float4_e2m1fn_x4
ACT = mybir.ActivationFunctionType
ALU = mybir.AluOpType

P = 128
PACK = 4
PASS = P * PACK
J_PASSES = J // PASS
M_TILE = 512
M_TILES = M // M_TILE
HALF = M_TILE // 2
N_TILES = N // P
LIST_COLS = PASS // 16

SIGN_AND_EXPONENT = -(1 << 23)
MANTISSA = (1 << 23) - 1
ONE_BITS = 127 << 23


def tile_list_kernl_exp_res_gelu_kernel(
    tc, x, tab_words, tab_scales, cw, cb, al4_words, al4_scales, al8_words, al8_scales, b, offs, out
):
    nc = tc.nc
    with ExitStack() as ctx:
        keep = ctx.enter_context(tc.tile_pool(name="keep", bufs=1))
        ring = ctx.enter_context(tc.tile_pool(name="ring", bufs=1))
        psum = ctx.enter_context(tc.psum_pool(name="psum", bufs=1))

        offsets = keep.tile([P, J // 16], U16, name="offsets")
        nc.sync.dma_start(offsets[:], offs)

        tab_s = keep.tile([P, T], U8, name="tab_s", align_bytes=64)
        nc.vector.memset(tab_s[:].bitcast(I32), 0)
        for q in (0, 2, 1, 3):
            nc.sync.dma_start(
                tab_s[32 * q : 32 * q + 4, :].bitcast(I32), tab_scales[0, 4 * q : 4 * q + 4, :].bitcast(I32)
            )

        cw_t = keep.tile([P, J_PASSES, PACK], F32, name="cw_t")
        cb_t = keep.tile([P, J_PASSES, PACK], F32, name="cb_t")
        nc.sync.dma_start(cw_t[:], cw.rearrange("(a p t) -> p a t", p=P, t=PACK))
        nc.sync.dma_start(cb_t[:], cb.rearrange("(a p t) -> p a t", p=P, t=PACK))

        x_view = x.rearrange("(p t) m -> p t m", t=PACK)
        x_raw = [keep.tile([P, PACK, M_TILE], F32, name=f"x_raw{mt}", align_bytes=64) for mt in range(M_TILES)]
        tab_w = keep.tile([P, T], I32, name="tab_w", align_bytes=64)
        nc.sync.dma_start(x_raw[0][:], x_view[:, :, 0:M_TILE])
        nc.sync.dma_start(tab_w[:], tab_words[0].rearrange("p t i -> p (t i)").bitcast(I32))
        nc.sync.dma_start(x_raw[1][:], x_view[:, :, M_TILE:M])

        al4_s = keep.tile([P, J_PASSES, N], U8, name="al4_s", align_bytes=64)
        al8_s = keep.tile([P, J_PASSES, N], U8, name="al8_s", align_bytes=64)
        nc.gpsimd.memset(al4_s[:].bitcast(I32), 0)
        nc.gpsimd.memset(al8_s[:].bitcast(I32), 0)
        al8_w = keep.tile([P, J_PASSES, N], I32, name="al8_w", align_bytes=64)
        al4_w = keep.tile([P, J_PASSES, N // 2], I32, name="al4_w", align_bytes=64)
        nc.sync.dma_start(al8_w[:], al8_words.rearrange("a p n i -> p a (n i)").bitcast(I32))
        nc.sync.dma_start(al4_w[:], al4_words.rearrange("a p c -> p a c").bitcast(I32))
        for plane, rows in ((al4_s, al4_scales), (al8_s, al8_scales)):
            for q in (0, 2, 1, 3):
                nc.sync.dma_start(
                    plane[32 * q : 32 * q + 4, :, :].bitcast(I32),
                    rows[:, 4 * q : 4 * q + 4, :].rearrange("a r n -> r a n").bitcast(I32),
                )
        b_t = keep.tile([P, N_TILES], F32, name="b_t")
        with nc.allow_non_contiguous_dma(reason="one bias value a partition"):
            nc.sync.dma_start(b_t[:], b.rearrange("(u p) -> p u", p=P))

        cw_bits = cw_t[:].rearrange("p a t -> p (a t)").bitcast(I32)
        power = keep.tile([P, J_PASSES * PACK], F32, name="power")
        mant = keep.tile([P, J_PASSES * PACK], F32, name="mant")
        nc.vector.tensor_scalar(mant[:].bitcast(I32), cw_bits, MANTISSA, ONE_BITS, ALU.bitwise_and, ALU.bitwise_or)
        nc.vector.tensor_scalar(power[:].bitcast(I32), cw_bits, SIGN_AND_EXPONENT, None, ALU.bitwise_and)
        power_bf = keep.tile([P, J_PASSES * PACK], BF16, name="power_bf")
        nc.vector.tensor_copy(power_bf[:], power[:])
        log_mant = keep.tile([P, J_PASSES * PACK], F32, name="log_mant")
        nc.scalar.activation(log_mant[:], mant[:], ACT.Ln)
        result_first = keep.tile([P, N_TILES, M_TILE], F32, name="result_first")
        result_last = keep.tile([P, 2, N_TILES, HALF], F32, name="result_last")
        shift = keep.tile([P, J_PASSES * PACK], F32, name="shift")
        nc.vector.tensor_tensor(shift[:], log_mant[:], cb_t[:].rearrange("p a t -> p (a t)"), ALU.subtract)
        steps = [(mt, a) for mt in range(M_TILES) for a in range(J_PASSES)]
        own_shift = {}
        for s in range(1, len(steps)):
            a = steps[s][1]
            holds = (("grouped", 1), ("codes", 3)) if s + 1 < len(steps) else (("grouped", 1), ("codes", 2), ("b", 3))
            for tag, t in holds:
                column = keep.tile([P, 1], F32, name=f"shift{s}{t}", tag=f"{tag}{s - 1}", align_bytes=64)
                nc.scalar.activation(
                    column[:],
                    cb_t[:, a, t : t + 1],
                    ACT.Identity,
                    bias=log_mant[:, a * PACK + t : a * PACK + t + 1],
                    scale=-1.0,
                )
                own_shift[s, t] = column[:]

        def gather_scales(a):
            picked = keep.tile([P, 2 * PASS], U8, name=f"picked_s{a}", align_bytes=64)
            nc.vector.tensor_copy(picked[:], tab_s[:].indirect(offsets[:, a * LIST_COLS : (a + 2) * LIST_COLS]))
            ordered = keep.tile([P, 2 * PASS], U8, name=f"v_s{a}", align_bytes=64)
            nc.vector.tensor_copy(
                ordered[:].rearrange("p (a t c i) -> p a c t i", a=2, t=PACK, i=16),
                picked[:].rearrange("p (a c i t) -> p a c t i", a=2, t=PACK, i=16),
            )
            return [ordered[:, 0:PASS], ordered[:, PASS:]]

        def gather_words(a):
            ordered = keep.tile([P, PASS], U32, name=f"v_w{a}", align_bytes=64)
            nc.vector.tensor_copy(
                ordered[:].rearrange("p (t q) -> p q t", t=PACK),
                tab_w[:].bitcast(U32).indirect(offsets[:, a * LIST_COLS : (a + 1) * LIST_COLS]),
            )
            return ordered

        def quantise_x(mt):
            grouped = keep.tile([P, M_TILE * PACK], BF16, name=f"x_bf{mt}", align_bytes=64)
            shares = [(nc.scalar.copy, 0, M_TILE)]
            if mt == 1:
                shares = [(nc.scalar.copy, 0, HALF), (nc.vector.tensor_copy, HALF, M_TILE)]
            for copy, lo, hi in shares:
                copy(
                    grouped[:, lo * PACK : hi * PACK].rearrange("p (c i t) -> p c t i", t=PACK, i=4),
                    x_raw[mt][:, :, lo:hi].rearrange("p t (c i) -> p c t i", i=4),
                )
            codes = keep.tile([P, M_TILE], U32, name=f"x_w{mt}", align_bytes=64)
            scales = keep.tile([P, M_TILE], U8, name=f"x_s{mt}", align_bytes=64)
            nc.vector.quantize_mx(codes[:].bitcast(FP8X4), scales[:], grouped[:])
            return codes, scales

        v_s = gather_scales(0) + gather_scales(2)
        x_q = [quantise_x(0)]
        v_w = [gather_words(0)]
        v_w.extend(gather_words(a) for a in range(1, J_PASSES))
        x_q.append(quantise_x(1))

        y_first = [psum.tile([P, M_TILE], F32, name=f"y_first{u}") for u in range(N_TILES)]
        y_last = [psum.tile([P, N_TILES, HALF], F32, name=f"y_last{h}") for h in range(2)]

        def first_stage(s):
            mt, a = steps[s]
            planes = ring.tile([P, PACK, M_TILE], BF16, name="h_planes", bufs=6, align_bytes=64)
            for t in range(PACK):
                d = psum.tile([P, M_TILE], F32, name=f"d{t}")
                cols = slice(t * P, (t + 1) * P)
                nc.tensor.matmul_mx(
                    d[:],
                    lhsT=v_w[a][:, cols].bitcast(FP8X4),
                    lhsT_scale=v_s[a][:, cols],
                    rhs=x_q[mt][0][:].bitcast(FP8X4),
                    rhs_scale=x_q[mt][1][:],
                    start=True,
                    stop=True,
                )
                bias = own_shift.get((s, t), shift[:, a * PACK + t : a * PACK + t + 1])
                nc.scalar.activation(planes[:, t, :], d[:], ACT.Exp, bias=bias)
            return planes

        def weigh(s, t, planes, weighed):
            col = steps[s][1] * PACK + t
            nc.vector.tensor_scalar(weighed[:, t, :], planes[:, t, :], power_bf[:, col : col + 1], None, ALU.mult)

        def interleave(weighed, lo, width, tag):
            grouped = keep.tile([P, width * PACK], BF16, name="grouped", tag=f"grouped{tag}", align_bytes=64)
            nc.vector.tensor_copy(
                grouped[:].rearrange("p (c i t) -> p c t i", t=PACK, i=4),
                weighed[:, :, lo : lo + width].rearrange("p t (c i) -> p c t i", i=4),
            )
            return grouped

        def product(target, a, u, codes, scales, fp4, start, stop):
            cols = slice(u * P, (u + 1) * P)
            if fp4:
                lhs, lhs_s = al4_w[:, a, u * P // 2 : (u + 1) * P // 2].bitcast(U8).bitcast(FP4X4), al4_s[:, a, cols]
            else:
                lhs, lhs_s = al8_w[:, a, cols].bitcast(FP8X4), al8_s[:, a, cols]
            nc.tensor.matmul_mx(
                target, lhsT=lhs, lhsT_scale=lhs_s, rhs=codes.bitcast(FP8X4), rhs_scale=scales, start=start, stop=stop
            )

        def second_stage(s, grouped, lo, width, tag):
            mt, a = steps[s]
            first, last = a == 0, a == J_PASSES - 1
            codes = keep.tile([P, width], U32, name="h_w", tag=f"codes{tag}", align_bytes=64)
            scales = ring.tile([P, M_TILE], U8, name="h_s", bufs=4, align_bytes=64)
            nc.vector.quantize_mx(codes[:].bitcast(FP8X4), scales[:, 0:width], grouped[:])
            if mt == 0:
                for u in range(N_TILES):
                    product(y_first[u][:], a, u, codes[:], scales[:], True, first, False)
                    product(y_first[u][:], a, u, codes[:], scales[:], False, False, last)
                return
            for half in range(lo // HALF, (lo + width) // HALF):
                base = half * HALF - lo
                for u in range(N_TILES):
                    for c in range(HALF // P):
                        src = slice(base + c * P, base + (c + 1) * P)
                        target = y_last[half][:, u, c * P : (c + 1) * P]
                        product(target, a, u, codes[:, src], scales[:, src], True, first and u == 0 and c == 0, False)
                    src = slice(base, base + HALF)
                    closes = last and u == N_TILES - 1
                    product(y_last[half][:, u, :], a, u, codes[:, src], scales[:, src], False, False, closes)

        weighed_prev = None
        for s in range(len(steps)):
            planes = first_stage(s)
            weighed = ring.tile([P, PACK, M_TILE], BF16, name="h_weighed", bufs=3, align_bytes=64)
            weigh(s, 0, planes, weighed)
            weigh(s, 1, planes, weighed)
            if s > 0:
                grouped = interleave(weighed_prev, 0, M_TILE, s - 1)
            weigh(s, 2, planes, weighed)
            if s + 1 < len(steps):
                weigh(s, 3, planes, weighed)
            if s > 0:
                second_stage(s - 1, grouped, 0, M_TILE, s - 1)
            weighed_prev = weighed
        weigh(len(steps) - 1, 3, planes, weighed)
        halves = [interleave(weighed, half * HALF, HALF, f"last{half}") for half in range(2)]
        for half in range(2):
            second_stage(len(steps) - 1, halves[half], half * HALF, HALF, f"last{half}")

        b_late = keep.tile([P, N_TILES], F32, name="b_late", tag=f"b{len(steps) - 2}", align_bytes=64)
        nc.scalar.copy(b_late[:], b_t[:])
        out_view = out.rearrange("(u p) m -> p u m", p=P)
        for u in range(N_TILES):
            nc.scalar.activation(result_first[:, u, :], y_first[u][:], ACT.Gelu_apprx_tanh, bias=b_late[:, u : u + 1])
        nc.sync.dma_start(out_view[:, :, 0:M_TILE], result_first[:])
        for half in range(2):
            for u in range(N_TILES):
                nc.scalar.activation(
                    result_last[:, half, u, :], y_last[half][:, u, :], ACT.Gelu_apprx_tanh, bias=b_late[:, u : u + 1]
                )
                lo = M_TILE + half * HALF
                nc.sync.dma_start(out_view[:, u, lo : lo + HALF], result_last[:, half, u, :])
